import numpy as np
import ml_dtypes


def mxq(x, axis, fmt="e4m3"):
    dtype, down = {"e4m3": (ml_dtypes.float8_e4m3fn, 7), "e5m2": (ml_dtypes.float8_e5m2, 14)}[fmt]
    v = np.moveaxis(np.asarray(x, np.float32).astype(ml_dtypes.bfloat16).astype(np.float64), axis, -1)
    blocks = v.reshape(v.shape[:-1] + (-1, 32))
    amax = np.abs(blocks).max(-1, keepdims=True)
    byte = np.maximum(np.where(amax > 0, np.frexp(amax)[1] - 1 + 127, 0) - down, 1)
    scale = np.exp2(byte - 127.0)
    codes = (blocks / scale).astype(np.float32).astype(dtype).astype(np.float64)
    return np.moveaxis((codes * scale).reshape(v.shape), -1, axis)


WIDE = False


def mx_kscale(k):
    if not WIDE:
        return np.ones(k)
    levels = np.array([10, -10, 5, -5, 0])
    if k % 512:
        return np.exp2(np.random.permutation(np.resize(levels, k // 32))).repeat(32)
    a = np.empty((k // 512, 16))
    for p in range(k // 512):
        a[p, :8] = np.random.permutation(np.resize(levels, 8))
        for g in range(8):
            far = levels[np.abs(levels - a[p, g]) >= 10]
            a[p, g + 8] = far[np.random.randint(len(far))]
    return np.exp2(a.ravel()).repeat(32)


def f64(x):
    return np.asarray(x).astype(np.float64)


def striped(idx):
    return np.tile(idx.reshape(-1, 16).T, (8, 1)).astype(np.uint16)


def unstriped(offs):
    return offs[:16].T.reshape(-1).astype(np.int64)


def striped8(idx):
    return np.concatenate([x.reshape(-1, 16).T for x in idx]).astype(np.uint16)


def runs(offs, k):
    lists = np.stack([offs[16 * r : 16 * r + 16].T.reshape(-1) for r in range(8)]).astype(np.int64)
    return lists[np.arange(k) % 512 // 64]


def pack_weight(w):
    k, n = w.shape
    w = f64(np.asarray(w, np.float32).astype(ml_dtypes.bfloat16)).reshape(k // 32, 32, n)
    amax = np.abs(w).max(1)
    byte = np.clip(np.where(amax > 0, np.frexp(amax)[1] - 1 + 127 - 7, 1), 1, 254)
    scaled = (w * np.exp2(127.0 - byte)[:, None, :]).reshape(k, n).astype(np.float32)
    words = np.ascontiguousarray(scaled.reshape(k // 512, 128, 4, n).transpose(0, 1, 3, 2)).astype(ml_dtypes.float8_e4m3fn).view(np.uint8)
    return words, np.ascontiguousarray(byte.astype(np.uint8).reshape(k // 512, 16, n))


def unpack_weight(words, scales):
    g, p, n, _ = words.shape
    vals = np.ascontiguousarray(words).view(ml_dtypes.float8_e4m3fn).astype(np.float64) * np.repeat(np.exp2(scales.astype(np.float64) - 127.0), 8, axis=1)[..., None]
    return vals.transpose(0, 1, 3, 2).reshape(g * 512, n)


K, T, S, H, G, W = 512, 1024, 256, 512, 2048, 128


def setup_inputs():
    n = np.random.standard_normal
    s = mx_kscale(K)[:, None]
    packed_xT = pack_weight(n((K, T)) * s)
    packed_dT = pack_weight(n((K, G)) / s)
    perm = np.random.permutation(S)
    return {
        "x_words": packed_xT[0],
        "x_scales": packed_xT[1],
        "w1": (n((K, H)) / np.sqrt(K) / s).astype(np.float32),
        "gs": (np.random.uniform(0.5, 1.5, (K, 1)) * s).astype(np.float32),
        "d_words": packed_dT[0],
        "d_scales": packed_dT[1],
        "offs": striped(np.random.permutation(T)[:S]),
        "k1": striped8(np.random.randint(0, G, (8, H))),
        "k2": striped8(np.random.randint(0, G, (8, H))),
        "two": striped(np.random.permutation(T)[:S]),
        "n1": striped(perm[:W]),
        "n2": striped(perm[W:]),
        "n3": striped(np.random.permutation(S)),
    }


def reference(x_words, x_scales, w1, gs, d_words, d_scales, offs, k1, k2, two, n1, n2, n3):
    d_k1 = unpack_weight(d_words, d_scales)[np.arange(K)[:, None], runs(k1, K)]
    xq = unpack_weight(x_words, x_scales)[:, unstriped(offs)]
    y = mxq(f64(w1), 0, "e4m3").T @ xq
    z = f64(gs) * y
    d_k2 = unpack_weight(d_words, d_scales)[np.arange(K)[:, None], runs(k2, K)]
    x_two = unpack_weight(x_words, x_scales)[:, unstriped(two)]
    h = 0.0625 * ((d_k1.T @ mxq(z, 0, "e4m3") + d_k2.T @ x_two))
    pa = h[:, unstriped(n1)]
    pb = h[:, unstriped(n2)]
    rb = pa - pb
    ds = np.zeros((H, S))
    ds[:, unstriped(n1)] = pb
    dt = ds.copy()
    dt[:, unstriped(n2)] = rb
    return np.maximum(dt, 0.5 * dt[:, unstriped(n3)])

@@ -1,0 +1,201 @@
+from contextlib import ExitStack
+
+import concourse.mybir as mybir
+
+K, T, S, H, G, W = 512, 1024, 256, 512, 2048, 128
+P = 128
+FLOPS = 3 * 2 * K * H * S
+
+F32 = mybir.dt.float32
+BF16 = mybir.dt.bfloat16
+I32 = mybir.dt.int32
+U32 = mybir.dt.uint32
+U16 = mybir.dt.uint16
+U8 = mybir.dt.uint8
+FP8X4 = mybir.dt.float8_e4m3fn_x4
+ALU = mybir.AluOpType
+COPY = mybir.ActivationFunctionType.Copy
+
+
+def tile_picked_cmixiswapd_none_p_kernel(
+    tc, x_words, x_scales, w1, gs, d_words, d_scales, offs, k1, k2, two, n1, n2, n3, out
+):
+    nc = tc.nc
+    with ExitStack() as ctx:
+        sb = ctx.enter_context(tc.tile_pool(name="sb", bufs=1))
+        ps = ctx.enter_context(tc.psum_pool(name="ps", bufs=1))
+
+        def sbuf(name, shape, dtype, tag=None):
+            return sb.tile(shape, dtype, name=name, tag=tag or name, align_bytes=64)
+
+        def load_list(name, src):
+            t = sbuf(name, [P, src.shape[1]], U16)
+            nc.sync.dma_start(t[:], src)
+            return t
+
+        xs_win = sbuf("xs_win", [P, T], U8)
+        ds_win = sbuf("ds_win", [P, G], U8)
+        nc.vector.memset(ds_win[:].bitcast(I32), 0)
+        nc.vector.memset(xs_win[:].bitcast(I32), 0)
+
+        w_raw = [sbuf(f"w_raw{c}", [P, 4, H // 2], F32) for c in range(2)]
+        xw_win = sbuf("xw_win", [P, T], U32)
+        dw_win = sbuf("dw_win", [P, G], U32)
+        w_rows = w1.rearrange("(p j) c -> p j c", j=4)
+
+        nc.sync.dma_start(w_raw[0][:], w_rows[:, :, 0 : H // 2])
+        k1_t = load_list("k1_t", k1)
+        for j in range(2):
+            nc.sync.dma_start(ds_win[j:P:16, :].bitcast(I32), d_scales[0][j:16:2, :].bitcast(I32))
+        k2_t = load_list("k2_t", k2)
+        nc.sync.dma_start(w_raw[1][:], w_rows[:, :, H // 2 : H])
+        offs_t = load_list("offs_t", offs)
+        nc.sync.dma_start(xw_win[:].bitcast(I32), x_words[0].rearrange("p n t -> p (n t)").bitcast(I32))
+        for q in range(4):
+            nc.sync.dma_start(
+                xs_win[32 * q : 32 * q + 4, :].bitcast(I32), x_scales[0][4 * q : 4 * q + 4, :].bitcast(I32)
+            )
+        nc.sync.dma_start(dw_win[:].bitcast(I32), d_words[0].rearrange("p n t -> p (n t)").bitcast(I32))
+        two_t = load_list("two_t", two)
+        gs_t = sbuf("gs_t", [P, 4], F32)
+        nc.gpsimd.dma_start(gs_t[:], gs.rearrange("(p t) o -> p (t o)", t=4))
+        n2_t = load_list("n2_t", n2)
+        n1_t = load_list("n1_t", n1)
+        n3_t = load_list("n3_t", n3)
+
+        ds_got = sbuf("ds_got", [P, 2 * H], U8)
+        ds_plane = sbuf("ds_plane", [P, 2 * H], U8)
+        nc.vector.tensor_copy(ds_got[:, 0:H], ds_win[:].indirect(k1_t[:]))
+        nc.vector.tensor_copy(ds_got[:, H : 2 * H], ds_win[:].indirect(k2_t[:]))
+        xq_s = sbuf("xq_s", [P, S], U8)
+        nc.vector.tensor_copy(xq_s[:], xs_win[:].indirect(offs_t[:]))
+        nc.vector.tensor_copy(ds_plane[:].bitcast(I32), ds_got[:].bitcast(I32))
+        for j in range(2):
+            nc.sync.dma_start(ds_plane[2 + j : P : 32, :].bitcast(I32), ds_got[16 + j : P : 32, :].bitcast(I32))
+
+        xq_w = sbuf("xq_w", [P, S], U32)
+        nc.vector.tensor_copy(xq_w[:], xw_win[:].indirect(offs_t[:]))
+        x2_s = sbuf("x2_s", [P, S], U8)
+        x2_w = sbuf("x2_w", [P, S], U32)
+        nc.vector.tensor_copy(x2_s[:], xs_win[:].indirect(two_t[:]))
+
+        w_bf = sbuf("w_bf", [P, 4, P, 4], BF16)
+        for c in range(2):
+            nc.scalar.copy(
+                w_bf[:, :, 64 * c : 64 * c + 64, :].rearrange("p t m j -> p m j t"),
+                w_raw[c][:].rearrange("p j (m t) -> p m j t", t=4),
+            )
+        w_q = sbuf("w_q", [P, H], U32)
+        w_s = sbuf("w_s", [P, H], U8)
+        y_ps = [ps.tile([P, 4, P], F32, name=f"y_ps{c}") for c in range(2)]
+        for t in range(4):
+            cols = slice(P * t, P * t + P)
+            nc.vector.quantize_mx(
+                out=w_q[:, cols].bitcast(FP8X4), scales=w_s[:, cols], in_=w_bf[:, t].rearrange("p m j -> p (m j)")
+            )
+            for c in range(2):
+                tok = slice(P * c, P * c + P)
+                nc.tensor.matmul_mx(
+                    out=y_ps[c][:, t, :],
+                    lhsT=w_q[:, cols].bitcast(FP8X4),
+                    lhsT_scale=w_s[:, cols],
+                    rhs=xq_w[:, tok].bitcast(FP8X4),
+                    rhs_scale=xq_s[:, tok],
+                    start=True,
+                    stop=True,
+                )
+        nc.vector.tensor_copy(x2_w[:], xw_win[:].indirect(two_t[:]))
+
+        z_bf = [sbuf(f"z_bf{c}", [P, P, 4], BF16) for c in range(2)]
+        z_q = sbuf("z_q", [P, S], U32)
+        z_s = sbuf("z_s", [P, S], U8)
+        d1_w, d2_w = [None, None], [None, None]
+
+        def gather_words(dst, lists, u, name, tag=None):
+            dst[u] = sbuf(name, [P, H // 2], U32, tag)
+            nc.vector.tensor_copy(dst[u][:], dw_win[:].indirect(lists[:, 16 * u : 16 * u + 16]))
+
+        for c in range(2):
+            nc.vector.tensor_tensor(
+                z_bf[c][:],
+                y_ps[c][:].rearrange("p t n -> p n t"),
+                gs_t[:].unsqueeze(1).to_broadcast([P, P, 4]),
+                ALU.mult,
+            )
+        gather_words(d2_w, k2_t, 0, "d2_w0")
+        for c in range(2):
+            tok = slice(P * c, P * c + P)
+            nc.vector.quantize_mx(
+                out=z_q[:, tok].bitcast(FP8X4), scales=z_s[:, tok], in_=z_bf[c][:].rearrange("p n t -> p (n t)")
+            )
+        gather_words(d1_w, k1_t, 0, "d1_w0")
+
+        nb = H // P
+        h_sb, pa, pb, rb, dt, got, res = ([None] * nb for i in range(7))
+
+        def product(b):
+            u, v = divmod(b, 2)
+            cols = slice(P * v, P * v + P)
+            h_ps = ps.tile([P, S], F32, name=f"h_ps{b}")
+            nc.tensor.matmul_mx(
+                out=h_ps[:],
+                lhsT=d2_w[u][:, cols].bitcast(FP8X4),
+                lhsT_scale=ds_plane[:, H + P * b : H + P * b + P],
+                rhs=x2_w[:].bitcast(FP8X4),
+                rhs_scale=x2_s[:],
+                start=True,
+                stop=False,
+            )
+            nc.tensor.matmul_mx(
+                out=h_ps[:],
+                lhsT=d1_w[u][:, cols].bitcast(FP8X4),
+                lhsT_scale=ds_plane[:, P * b : P * b + P],
+                rhs=z_q[:].bitcast(FP8X4),
+                rhs_scale=z_s[:],
+                start=False,
+                stop=True,
+            )
+            h_sb[b] = sbuf(f"h_sb{b}", [P, S], F32)
+            if b == 0:
+                nc.scalar.activation(h_sb[b][:], h_ps[:], COPY, scale=0.0625)
+            else:
+                nc.vector.tensor_scalar(h_sb[b][:], h_ps[:], 0.0625, None, ALU.mult)
+
+        def fetch_pairs(b):
+            pb[b] = sbuf(f"pb{b}", [P, W], F32)
+            pa[b] = sbuf(f"pa{b}", [P, W], F32)
+            rb[b] = sbuf(f"rb{b}", [P, W], F32)
+            nc.scalar.activation(pb[b][:], h_sb[b][:].indirect(n2_t[:]), COPY)
+            nc.scalar.activation(pa[b][:], h_sb[b][:].indirect(n1_t[:]), COPY)
+            nc.vector.tensor_tensor(rb[b][:], pa[b][:], pb[b][:], ALU.subtract)
+
+        def put_first(b):
+            dt[b] = sbuf(f"dt{b}", [P, S], F32)
+            nc.scalar.activation(dt[b][:].indirect(n1_t[:]), pb[b][:], COPY)
+
+        def put_second(b):
+            nc.scalar.activation(dt[b][:].indirect(n2_t[:]), rb[b][:], COPY)
+
+        def finish(b):
+            got[b] = sbuf(f"got{b}", [P, S], F32)
+            res[b] = sbuf(f"res{b}", [P, S], F32)
+            for c in range(2):
+                nc.scalar.activation(got[b][:, W * c : W * c + W], dt[b][:].indirect(n3_t[:, 8 * c : 8 * c + 8]), COPY)
+            nc.vector.scalar_tensor_tensor(res[b][:], got[b][:], 0.5, dt[b][:], ALU.mult, ALU.max)
+            nc.sync.dma_start(out[P * b : P * b + P, :], res[b][:])
+
+        product(0)
+        product(1)
+        fetch_pairs(0)
+        gather_words(d2_w, k2_t, 1, "d2_w1", "z_bf0")
+        gather_words(d1_w, k1_t, 1, "d1_w1", "z_bf1")
+        product(2)
+        product(3)
+        for b in range(nb):
+            put_first(b)
+            if b + 1 < nb:
+                fetch_pairs(b + 1)
+            put_second(b)
+            if b > 0:
+                finish(b - 1)
+        finish(nb - 1)

@@ -35,49 +35,55 @@ def tile_picked_cmixiswapd_none_p_kernel(
 
         xs_win = sbuf("xs_win", [P, T], U8)
         ds_win = sbuf("ds_win", [P, G], U8)
-        nc.vector.memset(ds_win[:].bitcast(I32), 0)
         nc.vector.memset(xs_win[:].bitcast(I32), 0)
+        nc.vector.memset(ds_win[:].bitcast(I32), 0)
 
+        half = H // 2
         w_raw = [sbuf(f"w_raw{c}", [P, 4, H // 2], F32) for c in range(2)]
         xw_win = sbuf("xw_win", [P, T], U32)
         dw_win = sbuf("dw_win", [P, G], U32)
         w_rows = w1.rearrange("(p j) c -> p j c", j=4)
 
-        nc.sync.dma_start(w_raw[0][:], w_rows[:, :, 0 : H // 2])
-        k1_t = load_list("k1_t", k1)
-        for j in range(2):
-            nc.sync.dma_start(ds_win[j:P:16, :].bitcast(I32), d_scales[0][j:16:2, :].bitcast(I32))
-        k2_t = load_list("k2_t", k2)
-        nc.sync.dma_start(w_raw[1][:], w_rows[:, :, H // 2 : H])
         offs_t = load_list("offs_t", offs)
         nc.sync.dma_start(xw_win[:].bitcast(I32), x_words[0].rearrange("p n t -> p (n t)").bitcast(I32))
         for q in range(4):
             nc.sync.dma_start(
                 xs_win[32 * q : 32 * q + 4, :].bitcast(I32), x_scales[0][4 * q : 4 * q + 4, :].bitcast(I32)
             )
-        nc.sync.dma_start(dw_win[:].bitcast(I32), d_words[0].rearrange("p n t -> p (n t)").bitcast(I32))
         two_t = load_list("two_t", two)
+        for c in range(2):
+            nc.sync.dma_start(w_raw[c][:], w_rows[:, :, half * c : half * c + half])
+        k1_t = load_list("k1_t", k1)
+        nc.sync.dma_start(ds_win[0:P:8, :].bitcast(I32), d_scales[0].bitcast(I32))
+        k2_t = load_list("k2_t", k2)
+        nc.sync.dma_start(dw_win[:].bitcast(I32), d_words[0].rearrange("p n t -> p (n t)").bitcast(I32))
         gs_t = sbuf("gs_t", [P, 4], F32)
-        nc.gpsimd.dma_start(gs_t[:], gs.rearrange("(p t) o -> p (t o)", t=4))
+        nc.sync.dma_start(gs_t[:], gs.rearrange("(p t) o -> p (t o)", t=4))
+
+        xq_w = sbuf("xq_w", [P, S], U32)
+        x2_w = sbuf("x2_w", [P, S], U32)
+        nc.vector.tensor_copy(xq_w[:], xw_win[:].indirect(offs_t[:]))
+        xq_s = sbuf("xq_s", [P, S], U8)
+        x2_s = sbuf("x2_s", [P, S], U8)
+        nc.vector.tensor_copy(xq_s[:], xs_win[:].indirect(offs_t[:]))
+        nc.vector.tensor_copy(x2_s[:], xs_win[:].indirect(two_t[:]))
+        nc.vector.tensor_copy(x2_w[:], xw_win[:].indirect(two_t[:]))
+
+        ds_plane = [None, None]
+
+        def gather_scales(u, tag=None):
+            ds_got = sbuf(f"ds_got{u}", [P, H], U8, tag)
+            ds_plane[u] = sbuf(f"ds_plane{u}", [P, H], U8)
+            nc.vector.tensor_copy(ds_got[:, 0:half], ds_win[:].indirect(k1_t[:, 16 * u : 16 * u + 16]))
+            nc.vector.tensor_copy(ds_got[:, half:H], ds_win[:].indirect(k2_t[:, 16 * u : 16 * u + 16]))
+            nc.vector.tensor_copy(ds_plane[u][:].bitcast(I32), ds_got[:].bitcast(I32))
+            for j in range(1, 4):
+                nc.sync.dma_start(ds_plane[u][j:P:32, :].bitcast(I32), ds_plane[u][8 * j : P : 32, :].bitcast(I32))
+
+        gather_scales(0)
         n2_t = load_list("n2_t", n2)
         n1_t = load_list("n1_t", n1)
         n3_t = load_list("n3_t", n3)
-
-        ds_got = sbuf("ds_got", [P, 2 * H], U8)
-        ds_plane = sbuf("ds_plane", [P, 2 * H], U8)
-        nc.vector.tensor_copy(ds_got[:, 0:H], ds_win[:].indirect(k1_t[:]))
-        nc.vector.tensor_copy(ds_got[:, H : 2 * H], ds_win[:].indirect(k2_t[:]))
-        xq_s = sbuf("xq_s", [P, S], U8)
-        nc.vector.tensor_copy(xq_s[:], xs_win[:].indirect(offs_t[:]))
-        nc.vector.tensor_copy(ds_plane[:].bitcast(I32), ds_got[:].bitcast(I32))
-        for j in range(2):
-            nc.sync.dma_start(ds_plane[2 + j : P : 32, :].bitcast(I32), ds_got[16 + j : P : 32, :].bitcast(I32))
-
-        xq_w = sbuf("xq_w", [P, S], U32)
-        nc.vector.tensor_copy(xq_w[:], xw_win[:].indirect(offs_t[:]))
-        x2_s = sbuf("x2_s", [P, S], U8)
-        x2_w = sbuf("x2_w", [P, S], U32)
-        nc.vector.tensor_copy(x2_s[:], xs_win[:].indirect(two_t[:]))
 
         w_bf = sbuf("w_bf", [P, 4, P, 4], BF16)
         for c in range(2):
@@ -86,7 +92,7 @@ def tile_picked_cmixiswapd_none_p_kernel(
                 w_raw[c][:].rearrange("p j (m t) -> p m j t", t=4),
             )
         w_q = sbuf("w_q", [P, H], U32)
-        w_s = sbuf("w_s", [P, H], U8)
+        w_s = sbuf("w_s", [P, H], U8, "ds_got0")
         y_ps = [ps.tile([P, 4, P], F32, name=f"y_ps{c}") for c in range(2)]
         for t in range(4):
             cols = slice(P * t, P * t + P)
@@ -104,31 +110,34 @@ def tile_picked_cmixiswapd_none_p_kernel(
                     start=True,
                     stop=True,
                 )
-        nc.vector.tensor_copy(x2_w[:], xw_win[:].indirect(two_t[:]))
 
         z_bf = [sbuf(f"z_bf{c}", [P, P, 4], BF16) for c in range(2)]
         z_q = sbuf("z_q", [P, S], U32)
         z_s = sbuf("z_s", [P, S], U8)
-        d1_w, d2_w = [None, None], [None, None]
+        d_w = [sbuf("d_w0", [P, H], U32), None]
 
-        def gather_words(dst, lists, u, name, tag=None):
-            dst[u] = sbuf(name, [P, H // 2], U32, tag)
-            nc.vector.tensor_copy(dst[u][:], dw_win[:].indirect(lists[:, 16 * u : 16 * u + 16]))
+        def gather_words(lists, u, at):
+            nc.vector.tensor_copy(d_w[u][:, at : at + half], dw_win[:].indirect(lists[:, 16 * u : 16 * u + 16]))
 
-        for c in range(2):
-            nc.vector.tensor_tensor(
-                z_bf[c][:],
-                y_ps[c][:].rearrange("p t n -> p n t"),
-                gs_t[:].unsqueeze(1).to_broadcast([P, P, 4]),
-                ALU.mult,
-            )
-        gather_words(d2_w, k2_t, 0, "d2_w0")
-        for c in range(2):
+        gather_words(k2_t, 0, half)
+        gather_words(k1_t, 0, 0)
+        z_rows = sbuf("z_rows", [P, 4, P], BF16)
+        for t in range(4):
+            nc.scalar.activation(z_rows[:, t, :], y_ps[0][:, t, :], COPY, scale=gs_t[:, t : t + 1])
+        nc.scalar.copy(
+            z_bf[0][:].rearrange("p (c i) t -> p c t i", i=4), z_rows[:].rearrange("p t (c i) -> p c t i", i=4)
+        )
+        nc.vector.tensor_tensor(
+            z_bf[1][:],
+            y_ps[1][:].rearrange("p t n -> p n t"),
+            gs_t[:].unsqueeze(1).to_broadcast([P, P, 4]),
+            ALU.mult,
+        )
+        for c in (1, 0):
             tok = slice(P * c, P * c + P)
             nc.vector.quantize_mx(
                 out=z_q[:, tok].bitcast(FP8X4), scales=z_s[:, tok], in_=z_bf[c][:].rearrange("p n t -> p (n t)")
             )
-        gather_words(d1_w, k1_t, 0, "d1_w0")
 
         nb = H // P
         h_sb, pa, pb, rb, dt, got, res = ([None] * nb for i in range(7))
@@ -136,11 +145,12 @@ def tile_picked_cmixiswapd_none_p_kernel(
         def product(b):
             u, v = divmod(b, 2)
             cols = slice(P * v, P * v + P)
+            cols2 = slice(half + P * v, half + P * v + P)
             h_ps = ps.tile([P, S], F32, name=f"h_ps{b}")
             nc.tensor.matmul_mx(
                 out=h_ps[:],
-                lhsT=d2_w[u][:, cols].bitcast(FP8X4),
-                lhsT_scale=ds_plane[:, H + P * b : H + P * b + P],
+                lhsT=d_w[u][:, cols2].bitcast(FP8X4),
+                lhsT_scale=ds_plane[u][:, cols2],
                 rhs=x2_w[:].bitcast(FP8X4),
                 rhs_scale=x2_s[:],
                 start=True,
@@ -148,8 +158,8 @@ def tile_picked_cmixiswapd_none_p_kernel(
             )
             nc.tensor.matmul_mx(
                 out=h_ps[:],
-                lhsT=d1_w[u][:, cols].bitcast(FP8X4),
-                lhsT_scale=ds_plane[:, P * b : P * b + P],
+                lhsT=d_w[u][:, cols].bitcast(FP8X4),
+                lhsT_scale=ds_plane[u][:, cols],
                 rhs=z_q[:].bitcast(FP8X4),
                 rhs_scale=z_s[:],
                 start=False,
@@ -176,26 +186,41 @@ def tile_picked_cmixiswapd_none_p_kernel(
         def put_second(b):
             nc.scalar.activation(dt[b][:].indirect(n2_t[:]), rb[b][:], COPY)
 
-        def finish(b):
-            got[b] = sbuf(f"got{b}", [P, S], F32)
-            res[b] = sbuf(f"res{b}", [P, S], F32)
-            for c in range(2):
-                nc.scalar.activation(got[b][:, W * c : W * c + W], dt[b][:].indirect(n3_t[:, 8 * c : 8 * c + 8]), COPY)
-            nc.vector.scalar_tensor_tensor(res[b][:], got[b][:], 0.5, dt[b][:], ALU.mult, ALU.max)
-            nc.sync.dma_start(out[P * b : P * b + P, :], res[b][:])
+        def fetch_partner(b, c):
+            if c == 0:
+                got[b] = sbuf(f"got{b}", [P, S], F32)
+                res[b] = sbuf(f"res{b}", [P, S], F32, "pa0" if b == 0 else None)
+            nc.scalar.activation(got[b][:, W * c : W * c + W], dt[b][:].indirect(n3_t[:, 8 * c : 8 * c + 8]), COPY)
+
+        def store(b, cols):
+            nc.vector.scalar_tensor_tensor(res[b][:, cols], got[b][:, cols], 0.5, dt[b][:, cols], ALU.mult, ALU.max)
+            nc.sync.dma_start(out[P * b : P * b + P, cols], res[b][:, cols])
 
         product(0)
         product(1)
+        gather_scales(1, "ds_plane0")
         fetch_pairs(0)
-        gather_words(d2_w, k2_t, 1, "d2_w1", "z_bf0")
-        gather_words(d1_w, k1_t, 1, "d1_w1", "z_bf1")
+        put_first(0)
+        d_w[1] = sbuf("d_w1", [P, H], U32, "pa0")
+        gather_words(k2_t, 1, half)
+        gather_words(k1_t, 1, 0)
+        fetch_pairs(1)
+        put_second(0)
+        put_first(1)
         product(2)
         product(3)
-        for b in range(nb):
-            put_first(b)
-            if b + 1 < nb:
-                fetch_pairs(b + 1)
-            put_second(b)
-            if b > 0:
-                finish(b - 1)
-        finish(nb - 1)
+        for b in range(nb - 1):
+            fetch_partner(b, 0)
+            if b + 2 < nb:
+                fetch_partner(b, 1)
+                store(b, slice(0, S))
+                put_second(b + 1)
+                fetch_pairs(b + 2)
+                put_first(b + 2)
+            else:
+                put_second(b + 1)
+                fetch_partner(b, 1)
+                store(b, slice(0, S))
+        for c in range(2):
+            fetch_partner(nb - 1, c)
+            store(nb - 1, slice(W * c, W * c + W))

@@ -4,6 +4,8 @@ import concourse.mybir as mybir
 
 K, T, S, H, G, W = 512, 1024, 256, 512, 2048, 128
 P = 128
+CAST_SPLIT = 32
+SPARE = 32
 FLOPS = 3 * 2 * K * H * S
 
 F32 = mybir.dt.float32
@@ -35,39 +37,35 @@ def tile_picked_cmixiswapd_none_p_kernel(
 
         xs_win = sbuf("xs_win", [P, T], U8)
         ds_win = sbuf("ds_win", [P, G], U8)
+        nc.gpsimd.memset(ds_win[:].bitcast(I32), 0)
         nc.vector.memset(xs_win[:].bitcast(I32), 0)
-        nc.vector.memset(ds_win[:].bitcast(I32), 0)
 
+        nb = H // P
+        dt = [sbuf(f"dt{b}", [P, S + SPARE], F32) for b in range(nb)]
+        for b in range(nb):
+            nc.gpsimd.memset(dt[b][:, S : S + SPARE], 0.0)
         half = H // 2
-        w_raw = [sbuf(f"w_raw{c}", [P, 4, H // 2], F32) for c in range(2)]
+        w_raw = sbuf("w_raw", [P, 4, H], F32)
         xw_win = sbuf("xw_win", [P, T], U32)
         dw_win = sbuf("dw_win", [P, G], U32)
-        w_rows = w1.rearrange("(p j) c -> p j c", j=4)
 
         offs_t = load_list("offs_t", offs)
-        nc.sync.dma_start(xw_win[:].bitcast(I32), x_words[0].rearrange("p n t -> p (n t)").bitcast(I32))
+        k1_t = load_list("k1_t", k1)
+        k2_t = load_list("k2_t", k2)
+        nc.sync.dma_start(ds_win[0:P:8, :].bitcast(I32), d_scales[0].bitcast(I32))
+        nc.sync.dma_start(w_raw[:], w1.rearrange("(p j) c -> p j c", j=4))
         for q in range(4):
             nc.sync.dma_start(
                 xs_win[32 * q : 32 * q + 4, :].bitcast(I32), x_scales[0][4 * q : 4 * q + 4, :].bitcast(I32)
             )
+        nc.sync.dma_start(xw_win[:].bitcast(I32), x_words[0].rearrange("p n t -> p (n t)").bitcast(I32))
         two_t = load_list("two_t", two)
-        for c in range(2):
-            nc.sync.dma_start(w_raw[c][:], w_rows[:, :, half * c : half * c + half])
-        k1_t = load_list("k1_t", k1)
-        nc.sync.dma_start(ds_win[0:P:8, :].bitcast(I32), d_scales[0].bitcast(I32))
-        k2_t = load_list("k2_t", k2)
         nc.sync.dma_start(dw_win[:].bitcast(I32), d_words[0].rearrange("p n t -> p (n t)").bitcast(I32))
+        n2_t = load_list("n2_t", n2)
         gs_t = sbuf("gs_t", [P, 4], F32)
         nc.sync.dma_start(gs_t[:], gs.rearrange("(p t) o -> p (t o)", t=4))
-
-        xq_w = sbuf("xq_w", [P, S], U32)
-        x2_w = sbuf("x2_w", [P, S], U32)
-        nc.vector.tensor_copy(xq_w[:], xw_win[:].indirect(offs_t[:]))
-        xq_s = sbuf("xq_s", [P, S], U8)
-        x2_s = sbuf("x2_s", [P, S], U8)
-        nc.vector.tensor_copy(xq_s[:], xs_win[:].indirect(offs_t[:]))
-        nc.vector.tensor_copy(x2_s[:], xs_win[:].indirect(two_t[:]))
-        nc.vector.tensor_copy(x2_w[:], xw_win[:].indirect(two_t[:]))
+        n1_t = load_list("n1_t", n1)
+        n3_t = load_list("n3_t", n3)
 
         ds_plane = [None, None]
 
@@ -78,22 +76,28 @@ def tile_picked_cmixiswapd_none_p_kernel(
             nc.vector.tensor_copy(ds_got[:, half:H], ds_win[:].indirect(k2_t[:, 16 * u : 16 * u + 16]))
             nc.vector.tensor_copy(ds_plane[u][:].bitcast(I32), ds_got[:].bitcast(I32))
             for j in range(1, 4):
-                nc.sync.dma_start(ds_plane[u][j:P:32, :].bitcast(I32), ds_plane[u][8 * j : P : 32, :].bitcast(I32))
+                nc.sync.dma_start(ds_plane[u][j:P:32, :].bitcast(I32), ds_got[8 * j : P : 32, :].bitcast(I32))
 
         gather_scales(0)
-        n2_t = load_list("n2_t", n2)
-        n1_t = load_list("n1_t", n1)
-        n3_t = load_list("n3_t", n3)
 
         w_bf = sbuf("w_bf", [P, 4, P, 4], BF16)
-        for c in range(2):
-            nc.scalar.copy(
-                w_bf[:, :, 64 * c : 64 * c + 64, :].rearrange("p t m j -> p m j t"),
-                w_raw[c][:].rearrange("p j (m t) -> p m j t", t=4),
-            )
-        w_q = sbuf("w_q", [P, H], U32)
-        w_s = sbuf("w_s", [P, H], U8, "ds_got0")
-        y_ps = [ps.tile([P, 4, P], F32, name=f"y_ps{c}") for c in range(2)]
+        w_dst = w_bf[:].rearrange("p t m j -> p m j t")
+        w_src = w_raw[:].rearrange("p j (m t) -> p m j t", t=4)
+        nc.vector.tensor_copy(w_dst[:, 0:CAST_SPLIT], w_src[:, 0:CAST_SPLIT])
+        nc.scalar.copy(w_dst[:, CAST_SPLIT:P], w_src[:, CAST_SPLIT:P])
+
+        xq_s = sbuf("xq_s", [P, S], U8)
+        xq_w = sbuf("xq_w", [P, S], U32)
+        x2_s = sbuf("x2_s", [P, S], U8)
+        x2_w = sbuf("x2_w", [P, S], U32)
+        nc.vector.tensor_copy(xq_s[:], xs_win[:].indirect(offs_t[:]))
+        nc.vector.tensor_copy(xq_w[:], xw_win[:].indirect(offs_t[:]))
+        nc.vector.tensor_copy(x2_w[:], xw_win[:].indirect(two_t[:]))
+        nc.vector.tensor_copy(x2_s[:], xs_win[:].indirect(two_t[:]))
+        w_q = sbuf("w_q", [P, H], U32, "xw_win")
+        w_s = sbuf("w_s", [P, H], U8)
+        y_lo = [ps.tile([P, 2, P], F32, name=f"y_lo{c}") for c in range(2)]
+        y_hi = ps.tile([P, 4, P], F32, name="y_hi")
         for t in range(4):
             cols = slice(P * t, P * t + P)
             nc.vector.quantize_mx(
@@ -102,7 +106,7 @@ def tile_picked_cmixiswapd_none_p_kernel(
             for c in range(2):
                 tok = slice(P * c, P * c + P)
                 nc.tensor.matmul_mx(
-                    out=y_ps[c][:, t, :],
+                    out=y_hi[:, t, :] if c else y_lo[t // 2][:, t % 2, :],
                     lhsT=w_q[:, cols].bitcast(FP8X4),
                     lhsT_scale=w_s[:, cols],
                     rhs=xq_w[:, tok].bitcast(FP8X4),
@@ -123,13 +127,13 @@ def tile_picked_cmixiswapd_none_p_kernel(
         gather_words(k1_t, 0, 0)
         z_rows = sbuf("z_rows", [P, 4, P], BF16)
         for t in range(4):
-            nc.scalar.activation(z_rows[:, t, :], y_ps[0][:, t, :], COPY, scale=gs_t[:, t : t + 1])
+            nc.scalar.activation(z_rows[:, t, :], y_lo[t // 2][:, t % 2, :], COPY, scale=gs_t[:, t : t + 1])
         nc.scalar.copy(
             z_bf[0][:].rearrange("p (c i) t -> p c t i", i=4), z_rows[:].rearrange("p t (c i) -> p c t i", i=4)
         )
         nc.vector.tensor_tensor(
             z_bf[1][:],
-            y_ps[1][:].rearrange("p t n -> p n t"),
+            y_hi[:].rearrange("p t n -> p n t"),
             gs_t[:].unsqueeze(1).to_broadcast([P, P, 4]),
             ALU.mult,
         )
@@ -139,8 +143,7 @@ def tile_picked_cmixiswapd_none_p_kernel(
                 out=z_q[:, tok].bitcast(FP8X4), scales=z_s[:, tok], in_=z_bf[c][:].rearrange("p n t -> p (n t)")
             )
 
-        nb = H // P
-        h_sb, pa, pb, rb, dt, got, res = ([None] * nb for i in range(7))
+        h_sb, pa, pb, rb, got, res = ([None] * nb for i in range(6))
 
         def product(b):
             u, v = divmod(b, 2)
@@ -180,17 +183,16 @@ def tile_picked_cmixiswapd_none_p_kernel(
             nc.vector.tensor_tensor(rb[b][:], pa[b][:], pb[b][:], ALU.subtract)
 
         def put_first(b):
-            dt[b] = sbuf(f"dt{b}", [P, S], F32)
             nc.scalar.activation(dt[b][:].indirect(n1_t[:]), pb[b][:], COPY)
 
         def put_second(b):
             nc.scalar.activation(dt[b][:].indirect(n2_t[:]), rb[b][:], COPY)
 
-        def fetch_partner(b, c):
-            if c == 0:
+        def fetch_partner(b, cols):
+            if cols.start == 0:
                 got[b] = sbuf(f"got{b}", [P, S], F32)
-                res[b] = sbuf(f"res{b}", [P, S], F32, "pa0" if b == 0 else None)
-            nc.scalar.activation(got[b][:, W * c : W * c + W], dt[b][:].indirect(n3_t[:, 8 * c : 8 * c + 8]), COPY)
+                res[b] = sbuf(f"res{b}", [P, S], F32, ("pa0", "ds_plane1", None, None)[b])
+            nc.scalar.activation(got[b][:, cols], dt[b][:].indirect(n3_t[:, cols.start // 16 : cols.stop // 16]), COPY)
 
         def store(b, cols):
             nc.vector.scalar_tensor_tensor(res[b][:, cols], got[b][:, cols], 0.5, dt[b][:, cols], ALU.mult, ALU.max)
@@ -198,7 +200,7 @@ def tile_picked_cmixiswapd_none_p_kernel(
 
         product(0)
         product(1)
-        gather_scales(1, "ds_plane0")
+        gather_scales(1, "z_bf0")
         fetch_pairs(0)
         put_first(0)
         d_w[1] = sbuf("d_w1", [P, H], U32, "pa0")
@@ -209,18 +211,17 @@ def tile_picked_cmixiswapd_none_p_kernel(
         put_first(1)
         product(2)
         product(3)
-        for b in range(nb - 1):
-            fetch_partner(b, 0)
-            if b + 2 < nb:
-                fetch_partner(b, 1)
-                store(b, slice(0, S))
-                put_second(b + 1)
-                fetch_pairs(b + 2)
-                put_first(b + 2)
-            else:
-                put_second(b + 1)
-                fetch_partner(b, 1)
-                store(b, slice(0, S))
-        for c in range(2):
-            fetch_partner(nb - 1, c)
-            store(nb - 1, slice(W * c, W * c + W))
+        whole, halves = slice(0, S), [slice(0, W), slice(W, S)]
+        for b in range(nb - 2):
+            fetch_partner(b, whole)
+            store(b, whole)
+            put_second(b + 1)
+            fetch_pairs(b + 2)
+            put_first(b + 2)
+        fetch_partner(nb - 2, halves[0])
+        put_second(nb - 1)
+        fetch_partner(nb - 2, halves[1])
+        store(nb - 2, whole)
+        for cols in halves:
+            fetch_partner(nb - 1, cols)
+            store(nb - 1, cols)

@@ -4,7 +4,7 @@ import concourse.mybir as mybir
 
 K, T, S, H, G, W = 512, 1024, 256, 512, 2048, 128
 P = 128
-CAST_SPLIT = 32
+CAST_SPLIT = 48
 SPARE = 32
 FLOPS = 3 * 2 * K * H * S
 
@@ -81,8 +81,8 @@ def tile_picked_cmixiswapd_none_p_kernel(
         gather_scales(0)
 
         w_bf = sbuf("w_bf", [P, 4, P, 4], BF16)
-        w_dst = w_bf[:].rearrange("p t m j -> p m j t")
-        w_src = w_raw[:].rearrange("p j (m t) -> p m j t", t=4)
+        w_dst = w_bf[:].rearrange("p t m j -> p m t j")
+        w_src = w_raw[:].rearrange("p j (m t) -> p m t j", t=4)
         nc.vector.tensor_copy(w_dst[:, 0:CAST_SPLIT], w_src[:, 0:CAST_SPLIT])
         nc.scalar.copy(w_dst[:, CAST_SPLIT:P], w_src[:, CAST_SPLIT:P])
 

from contextlib import ExitStack

import concourse.mybir as mybir

K, T, S, H, G, W = 512, 1024, 256, 512, 2048, 128
P = 128
CAST_SPLIT = 48
SPARE = 32
FLOPS = 3 * 2 * K * H * S

F32 = mybir.dt.float32
BF16 = mybir.dt.bfloat16
I32 = mybir.dt.int32
U32 = mybir.dt.uint32
U16 = mybir.dt.uint16
U8 = mybir.dt.uint8
FP8X4 = mybir.dt.float8_e4m3fn_x4
ALU = mybir.AluOpType
COPY = mybir.ActivationFunctionType.Copy


def tile_picked_cmixiswapd_none_p_kernel(
    tc, x_words, x_scales, w1, gs, d_words, d_scales, offs, k1, k2, two, n1, n2, n3, out
):
    nc = tc.nc
    with ExitStack() as ctx:
        sb = ctx.enter_context(tc.tile_pool(name="sb", bufs=1))
        ps = ctx.enter_context(tc.psum_pool(name="ps", bufs=1))

        def sbuf(name, shape, dtype, tag=None):
            return sb.tile(shape, dtype, name=name, tag=tag or name, align_bytes=64)

        def load_list(name, src):
            t = sbuf(name, [P, src.shape[1]], U16)
            nc.sync.dma_start(t[:], src)
            return t

        xs_win = sbuf("xs_win", [P, T], U8)
        ds_win = sbuf("ds_win", [P, G], U8)
        nc.gpsimd.memset(ds_win[:].bitcast(I32), 0)
        nc.vector.memset(xs_win[:].bitcast(I32), 0)

        nb = H // P
        dt = [sbuf(f"dt{b}", [P, S + SPARE], F32) for b in range(nb)]
        for b in range(nb):
            nc.gpsimd.memset(dt[b][:, S : S + SPARE], 0.0)
        half = H // 2
        w_raw = sbuf("w_raw", [P, 4, H], F32)
        xw_win = sbuf("xw_win", [P, T], U32)
        dw_win = sbuf("dw_win", [P, G], U32)

        offs_t = load_list("offs_t", offs)
        k1_t = load_list("k1_t", k1)
        k2_t = load_list("k2_t", k2)
        nc.sync.dma_start(ds_win[0:P:8, :].bitcast(I32), d_scales[0].bitcast(I32))
        nc.sync.dma_start(w_raw[:], w1.rearrange("(p j) c -> p j c", j=4))
        for q in range(4):
            nc.sync.dma_start(
                xs_win[32 * q : 32 * q + 4, :].bitcast(I32), x_scales[0][4 * q : 4 * q + 4, :].bitcast(I32)
            )
        nc.sync.dma_start(xw_win[:].bitcast(I32), x_words[0].rearrange("p n t -> p (n t)").bitcast(I32))
        two_t = load_list("two_t", two)
        nc.sync.dma_start(dw_win[:].bitcast(I32), d_words[0].rearrange("p n t -> p (n t)").bitcast(I32))
        n2_t = load_list("n2_t", n2)
        gs_t = sbuf("gs_t", [P, 4], F32)
        nc.sync.dma_start(gs_t[:], gs.rearrange("(p t) o -> p (t o)", t=4))
        n1_t = load_list("n1_t", n1)
        n3_t = load_list("n3_t", n3)

        ds_plane = [None, None]

        def gather_scales(u, tag=None):
            ds_got = sbuf(f"ds_got{u}", [P, H], U8, tag)
            ds_plane[u] = sbuf(f"ds_plane{u}", [P, H], U8)
            nc.vector.tensor_copy(ds_got[:, 0:half], ds_win[:].indirect(k1_t[:, 16 * u : 16 * u + 16]))
            nc.vector.tensor_copy(ds_got[:, half:H], ds_win[:].indirect(k2_t[:, 16 * u : 16 * u + 16]))
            nc.vector.tensor_copy(ds_plane[u][:].bitcast(I32), ds_got[:].bitcast(I32))
            for j in range(1, 4):
                nc.sync.dma_start(ds_plane[u][j:P:32, :].bitcast(I32), ds_got[8 * j : P : 32, :].bitcast(I32))

        gather_scales(0)

        w_bf = sbuf("w_bf", [P, 4, P, 4], BF16)
        w_dst = w_bf[:].rearrange("p t m j -> p m t j")
        w_src = w_raw[:].rearrange("p j (m t) -> p m t j", t=4)
        nc.vector.tensor_copy(w_dst[:, 0:CAST_SPLIT], w_src[:, 0:CAST_SPLIT])
        nc.scalar.copy(w_dst[:, CAST_SPLIT:P], w_src[:, CAST_SPLIT:P])

        xq_s = sbuf("xq_s", [P, S], U8)
        xq_w = sbuf("xq_w", [P, S], U32)
        x2_s = sbuf("x2_s", [P, S], U8)
        x2_w = sbuf("x2_w", [P, S], U32)
        nc.vector.tensor_copy(xq_s[:], xs_win[:].indirect(offs_t[:]))
        nc.vector.tensor_copy(xq_w[:], xw_win[:].indirect(offs_t[:]))
        nc.vector.tensor_copy(x2_w[:], xw_win[:].indirect(two_t[:]))
        nc.vector.tensor_copy(x2_s[:], xs_win[:].indirect(two_t[:]))
        w_q = sbuf("w_q", [P, H], U32, "xw_win")
        w_s = sbuf("w_s", [P, H], U8)
        y_lo = [ps.tile([P, 2, P], F32, name=f"y_lo{c}") for c in range(2)]
        y_hi = ps.tile([P, 4, P], F32, name="y_hi")
        for t in range(4):
            cols = slice(P * t, P * t + P)
            nc.vector.quantize_mx(
                out=w_q[:, cols].bitcast(FP8X4), scales=w_s[:, cols], in_=w_bf[:, t].rearrange("p m j -> p (m j)")
            )
            for c in range(2):
                tok = slice(P * c, P * c + P)
                nc.tensor.matmul_mx(
                    out=y_hi[:, t, :] if c else y_lo[t // 2][:, t % 2, :],
                    lhsT=w_q[:, cols].bitcast(FP8X4),
                    lhsT_scale=w_s[:, cols],
                    rhs=xq_w[:, tok].bitcast(FP8X4),
                    rhs_scale=xq_s[:, tok],
                    start=True,
                    stop=True,
                )

        z_bf = [sbuf(f"z_bf{c}", [P, P, 4], BF16) for c in range(2)]
        z_q = sbuf("z_q", [P, S], U32)
        z_s = sbuf("z_s", [P, S], U8)
        d_w = [sbuf("d_w0", [P, H], U32), None]

        def gather_words(lists, u, at):
            nc.vector.tensor_copy(d_w[u][:, at : at + half], dw_win[:].indirect(lists[:, 16 * u : 16 * u + 16]))

        gather_words(k2_t, 0, half)
        gather_words(k1_t, 0, 0)
        z_rows = sbuf("z_rows", [P, 4, P], BF16)
        for t in range(4):
            nc.scalar.activation(z_rows[:, t, :], y_lo[t // 2][:, t % 2, :], COPY, scale=gs_t[:, t : t + 1])
        nc.scalar.copy(
            z_bf[0][:].rearrange("p (c i) t -> p c t i", i=4), z_rows[:].rearrange("p t (c i) -> p c t i", i=4)
        )
        nc.vector.tensor_tensor(
            z_bf[1][:],
            y_hi[:].rearrange("p t n -> p n t"),
            gs_t[:].unsqueeze(1).to_broadcast([P, P, 4]),
            ALU.mult,
        )
        for c in (1, 0):
            tok = slice(P * c, P * c + P)
            nc.vector.quantize_mx(
                out=z_q[:, tok].bitcast(FP8X4), scales=z_s[:, tok], in_=z_bf[c][:].rearrange("p n t -> p (n t)")
            )

        h_sb, pa, pb, rb, got, res = ([None] * nb for i in range(6))

        def product(b):
            u, v = divmod(b, 2)
            cols = slice(P * v, P * v + P)
            cols2 = slice(half + P * v, half + P * v + P)
            h_ps = ps.tile([P, S], F32, name=f"h_ps{b}")
            nc.tensor.matmul_mx(
                out=h_ps[:],
                lhsT=d_w[u][:, cols2].bitcast(FP8X4),
                lhsT_scale=ds_plane[u][:, cols2],
                rhs=x2_w[:].bitcast(FP8X4),
                rhs_scale=x2_s[:],
                start=True,
                stop=False,
            )
            nc.tensor.matmul_mx(
                out=h_ps[:],
                lhsT=d_w[u][:, cols].bitcast(FP8X4),
                lhsT_scale=ds_plane[u][:, cols],
                rhs=z_q[:].bitcast(FP8X4),
                rhs_scale=z_s[:],
                start=False,
                stop=True,
            )
            h_sb[b] = sbuf(f"h_sb{b}", [P, S], F32)
            if b == 0:
                nc.scalar.activation(h_sb[b][:], h_ps[:], COPY, scale=0.0625)
            else:
                nc.vector.tensor_scalar(h_sb[b][:], h_ps[:], 0.0625, None, ALU.mult)

        def fetch_pairs(b):
            pb[b] = sbuf(f"pb{b}", [P, W], F32)
            pa[b] = sbuf(f"pa{b}", [P, W], F32)
            rb[b] = sbuf(f"rb{b}", [P, W], F32)
            nc.scalar.activation(pb[b][:], h_sb[b][:].indirect(n2_t[:]), COPY)
            nc.scalar.activation(pa[b][:], h_sb[b][:].indirect(n1_t[:]), COPY)
            nc.vector.tensor_tensor(rb[b][:], pa[b][:], pb[b][:], ALU.subtract)

        def put_first(b):
            nc.scalar.activation(dt[b][:].indirect(n1_t[:]), pb[b][:], COPY)

        def put_second(b):
            nc.scalar.activation(dt[b][:].indirect(n2_t[:]), rb[b][:], COPY)

        def fetch_partner(b, cols):
            if cols.start == 0:
                got[b] = sbuf(f"got{b}", [P, S], F32)
                res[b] = sbuf(f"res{b}", [P, S], F32, ("pa0", "ds_plane1", None, None)[b])
            nc.scalar.activation(got[b][:, cols], dt[b][:].indirect(n3_t[:, cols.start // 16 : cols.stop // 16]), COPY)

        def store(b, cols):
            nc.vector.scalar_tensor_tensor(res[b][:, cols], got[b][:, cols], 0.5, dt[b][:, cols], ALU.mult, ALU.max)
            nc.sync.dma_start(out[P * b : P * b + P, cols], res[b][:, cols])

        product(0)
        product(1)
        gather_scales(1, "z_bf0")
        fetch_pairs(0)
        put_first(0)
        d_w[1] = sbuf("d_w1", [P, H], U32, "pa0")
        gather_words(k2_t, 1, half)
        gather_words(k1_t, 1, 0)
        fetch_pairs(1)
        put_second(0)
        put_first(1)
        product(2)
        product(3)
        whole, halves = slice(0, S), [slice(0, W), slice(W, S)]
        for b in range(nb - 2):
            fetch_partner(b, whole)
            store(b, whole)
            put_second(b + 1)
            fetch_pairs(b + 2)
            put_first(b + 2)
        fetch_partner(nb - 2, halves[0])
        put_second(nb - 1)
        fetch_partner(nb - 2, halves[1])
        store(nb - 2, whole)
        for cols in halves:
            fetch_partner(nb - 1, cols)
            store(nb - 1, cols)
